import numpy as np
import ml_dtypes


def mxq(x, axis, fmt="e4m3"):
    dtype, down = {"e4m3": (ml_dtypes.float8_e4m3fn, 7), "e5m2": (ml_dtypes.float8_e5m2, 14)}[fmt]
    v = np.moveaxis(np.asarray(x, np.float32).astype(ml_dtypes.bfloat16).astype(np.float64), axis, -1)
    blocks = v.reshape(v.shape[:-1] + (-1, 32))
    amax = np.abs(blocks).max(-1, keepdims=True)
    byte = np.maximum(np.where(amax > 0, np.frexp(amax)[1] - 1 + 127, 0) - down, 1)
    scale = np.exp2(byte - 127.0)
    codes = (blocks / scale).astype(np.float32).astype(dtype).astype(np.float64)
    return np.moveaxis((codes * scale).reshape(v.shape), -1, axis)


WIDE = False


def mx_kscale(k):
    if not WIDE:
        return np.ones(k)
    levels = np.array([10, -10, 5, -5, 0])
    if k % 512:
        return np.exp2(np.random.permutation(np.resize(levels, k // 32))).repeat(32)
    a = np.empty((k // 512, 16))
    for p in range(k // 512):
        a[p, :8] = np.random.permutation(np.resize(levels, 8))
        for g in range(8):
            far = levels[np.abs(levels - a[p, g]) >= 10]
            a[p, g + 8] = far[np.random.randint(len(far))]
    return np.exp2(a.ravel()).repeat(32)


def f64(x):
    return np.asarray(x).astype(np.float64)


def striped(idx):
    return np.tile(idx.reshape(-1, 16).T, (8, 1)).astype(np.uint16)


def unstriped(offs):
    return offs[:16].T.reshape(-1).astype(np.int64)


E2M1 = np.array([0.0, 0.5, 1.0, 1.5, 2.0, 3.0, 4.0, 6.0, -0.0, -0.5, -1.0, -1.5, -2.0, -3.0, -4.0, -6.0])


def pack_weight(w, fmt):
    k, n = w.shape
    w = f64(np.asarray(w, np.float32).astype(ml_dtypes.bfloat16)).reshape(k // 32, 32, n)
    amax = np.abs(w).max(1)
    if fmt == "e4m3":
        byte = np.frexp(amax)[1] - 1 + 127 - 7
    else:
        mant, ex = np.frexp(amax / 6.0)
        byte = np.where(mant > 0.5, ex, ex - 1) + 127
    byte = np.clip(np.where(amax > 0, byte, 1), 1, 254)
    scaled = (w * np.exp2(127.0 - byte)[:, None, :]).reshape(k, n).astype(np.float32)
    by_word = np.ascontiguousarray(scaled.reshape(k // 512, 128, 4, n).transpose(0, 1, 3, 2))
    if fmt == "e4m3":
        words = by_word.astype(ml_dtypes.float8_e4m3fn).view(np.uint8)
    else:
        c = by_word.astype(ml_dtypes.float4_e2m1fn).view(np.uint8) & 0xF
        words = (c[..., 0::2] | (c[..., 1::2] << 4)).reshape(k // 512, 128, 2 * n)
    return np.ascontiguousarray(words), np.ascontiguousarray(byte.astype(np.uint8).reshape(k // 512, 16, n))


def unpack_weight(words, scales, fmt):
    g, _, n = scales.shape
    words = np.ascontiguousarray(words).reshape(g, 128, n, -1)
    if fmt == "e4m3":
        vals = words.view(ml_dtypes.float8_e4m3fn).astype(np.float64)
    else:
        nib = np.empty((g, 128, n, 4), np.uint8)
        nib[..., 0::2] = words & 0xF
        nib[..., 1::2] = words >> 4
        vals = E2M1[nib]
    vals = vals * np.repeat(np.exp2(scales.astype(np.float64) - 127.0), 8, axis=1)[..., None]
    return vals.transpose(0, 1, 3, 2).reshape(g * 512, n)


def pack_table(v):
    words, scales = pack_weight(v, "e4m3")
    return np.concatenate([words.reshape(words.shape[0], -1), scales.reshape(scales.shape[0], -1)], axis=1)


def unpack_table(tab):
    g, t = tab.shape[0], tab.shape[1] // 528
    return unpack_weight(tab[:, :512 * t].reshape(g, 128, t, 4), tab[:, 512 * t:].reshape(g, 16, t), "e4m3")


K, H, M, T, S = 1536, 1024, 1024, 2048, 1024


def setup_inputs():
    n = np.random.standard_normal
    s = mx_kscale(K)[:, None]
    u = mx_kscale(H)[:, None]
    p_w2 = pack_weight(1.4 * n((H, M)) / np.sqrt(H) / u, "e2m1")
    return {
        "tab": pack_table(n((K, T)) * s),
        "w1": (n((K, H)) / np.sqrt(K) / s * u.T).astype(np.float32),
        "w2_words": p_w2[0],
        "w2_scales": p_w2[1],
        "prev": (n((1024, 1024))).astype(np.float32),
        "offs": striped(np.random.permutation(T)[:S]),
    }


def reference(tab, w1, w2_words, w2_scales, prev, offs):
    tab_ = unpack_table(tab)[:, unstriped(offs)]
    w1_ = mxq(f64(w1), 0, "e4m3")
    w2_ = unpack_weight(w2_words, w2_scales, "e2m1")
    h_ = mxq(np.maximum(w1_.T @ tab_, 0.0), 0, "e4m3")
    y = w2_.T @ h_
    return f64(prev) + y

@@ -1,0 +1,241 @@
+from contextlib import ExitStack
+
+import concourse.mybir as mybir
+
+K, H, M, T, S = 1536, 1024, 1024, 2048, 1024
+FLOPS = 2 * K * H * S + 2 * H * M * S
+
+F32 = mybir.dt.float32
+BF16 = mybir.dt.bfloat16
+I32 = mybir.dt.int32
+U32 = mybir.dt.uint32
+U16 = mybir.dt.uint16
+U8 = mybir.dt.uint8
+FP8X4 = mybir.dt.float8_e4m3fn_x4
+FP4X4 = mybir.dt.float4_e2m1fn_x4
+RELU = mybir.ActivationFunctionType.Relu
+ADD = mybir.AluOpType.add
+
+P = 128
+PASS = 512
+KA = K // PASS
+HB = H // PASS
+NS = S // 512
+NT = M // P
+
+
+def tile_list_tabmlp_res_kernel(tc, tab, w1, w2_words, w2_scales, prev, offs, out):
+    nc = tc.nc
+    with ExitStack() as ctx:
+        keep = ctx.enter_context(tc.tile_pool(name="keep", bufs=1))
+        ring = ctx.enter_context(tc.tile_pool(name="ring", bufs=3))
+        psum = ctx.enter_context(tc.psum_pool(name="psum", bufs=8))
+
+        offsets = keep.tile([P, S // 16], U16, name="offsets")
+        nc.sync.dma_start(offsets[:], offs)
+
+        tab_scales = keep.tile([P, T // 4], I32, name="tab_scales", align_bytes=64)
+        nc.vector.memset(tab_scales[:], 0)
+        w2_planes = keep.tile([P, HB, M // 4], I32, name="w2_planes", align_bytes=64)
+        nc.vector.memset(w2_planes[:], 0)
+        warm = keep.tile([P, 1], F32, name="warm")
+        nc.vector.memset(warm[:], 0.0)
+        nc.scalar.activation(warm[:], warm[:], RELU)
+
+        tab_bytes = tab[:, PASS * T :].rearrange("a (q t) -> a q t", t=T)
+
+        raw = {}
+        tab_words = {}
+
+        def load_w1(b, a):
+            raw[b, a] = keep.tile([P, 4, PASS], F32, name=f"raw_{b}_{a}")
+            nc.sync.dma_start(
+                raw[b, a][:],
+                w1[PASS * a : PASS * (a + 1), PASS * b : PASS * (b + 1)].rearrange("(p j) c -> p j c", j=4),
+            )
+
+        def load_tab(a):
+            tab_words[a] = keep.tile([P, T], I32, name=f"tab_words_{a}")
+            nc.sync.dma_start(
+                tab_words[a][:], tab[a, 0 : PASS * T].rearrange("(p x) -> p x", p=P).bitcast(I32)
+            )
+
+        load_w1(0, 0)
+        load_tab(0)
+        for q in range(4):
+            nc.sync.dma_start(
+                tab_scales[32 * q : 32 * q + 4 * KA, :],
+                tab_bytes[:, 4 * q : 4 * q + 4, :].bitcast(I32),
+            )
+        load_w1(0, 1)
+        load_tab(1)
+        load_tab(2)
+        load_w1(0, 2)
+        for a in range(KA):
+            load_w1(1, a)
+        w2_codes = {}
+        for b in range(HB):
+            w2_codes[b] = keep.tile([P, M // 2], I32, name=f"w2_codes_{b}", align_bytes=64)
+            nc.sync.dma_start(w2_codes[b][:], w2_words[b].bitcast(I32))
+        for q in range(4):
+            nc.sync.dma_start(
+                w2_planes[32 * q : 32 * q + 4, :, :],
+                w2_scales[:, 4 * q : 4 * q + 4, :].rearrange("b q n -> q b n").bitcast(I32),
+            )
+        prev_sb = {}
+        for s in range(NS):
+            for u in range(2):
+                prev_sb[s, u] = keep.tile([P, 4, 512], F32, name=f"prev_{s}_{u}")
+                nc.sync.dma_start(
+                    prev_sb[s, u][:],
+                    prev[512 * u : 512 * (u + 1), 512 * s : 512 * (s + 1)].rearrange("(t p) j -> p t j", p=P),
+                )
+
+        w1_codes = {}
+        w1_planes = {}
+
+        def lay_out_w1(b, a, on_scalar):
+            grouped = ring.tile([P, 4, P, 4], BF16, name="grouped", align_bytes=64)
+            src = raw[b, a][:].rearrange("p j (m t) -> p m j t", t=4)
+            dst = grouped[:].rearrange("p t m j -> p m j t")
+            if on_scalar > 0:
+                nc.scalar.copy(dst[:, :on_scalar], src[:, :on_scalar])
+            if on_scalar < P:
+                nc.vector.tensor_copy(dst[:, on_scalar:], src[:, on_scalar:])
+            return grouped
+
+        def quantize_w1(b, a, grouped):
+            w1_codes[b, a] = keep.tile([P, PASS], U32, name=f"w1_codes_{b}_{a}", align_bytes=64)
+            w1_planes[b, a] = keep.tile([P, PASS], U8, name=f"w1_planes_{b}_{a}", align_bytes=64)
+            nc.vector.quantize_mx(
+                out=w1_codes[b, a][:].bitcast(FP8X4),
+                scales=w1_planes[b, a][:],
+                in_=grouped[:].rearrange("p t m j -> p (t m j)"),
+            )
+
+        picked = {}
+        picked_scales = keep.tile([P, S], U8, name="picked_scales", align_bytes=64)
+
+        def gather_words(a, s):
+            if a not in picked:
+                picked[a] = keep.tile([P, S], U32, name=f"picked_{a}", align_bytes=64)
+            nc.vector.tensor_copy(
+                picked[a][:, 512 * s : 512 * (s + 1)],
+                tab_words[a][:].bitcast(U32).indirect(offsets[:, 32 * s : 32 * (s + 1)]),
+            )
+
+        def gather_scales(s):
+            nc.vector.tensor_copy(
+                picked_scales[:, 512 * s : 512 * (s + 1)],
+                tab_scales[:].bitcast(U8).indirect(offsets[:, 32 * s : 32 * (s + 1)]),
+            )
+
+        def layer1(dst, b, a, j, t0, n):
+            nc.tensor.matmul_mx(
+                out=dst,
+                lhsT=w1_codes[b, a][:, P * j : P * (j + 1)].bitcast(FP8X4),
+                lhsT_scale=w1_planes[b, a][:, P * j : P * (j + 1)],
+                rhs=picked[a][:, t0 : t0 + n].bitcast(FP8X4),
+                rhs_scale=picked_scales[4 * a : P, t0 : t0 + n],
+                start=(a == 0),
+                stop=(a == KA - 1),
+            )
+
+        h_grouped = {}
+        for b in range(HB):
+            for s in range(NS):
+                h_grouped[b, s] = keep.tile([P, 512, 4], BF16, name=f"h_grouped_{b}_{s}", align_bytes=64)
+        h_codes = {}
+        h_planes = {}
+        for b in range(HB):
+            for s in range(NS):
+                h_codes[b, s] = keep.tile([P, 512], U32, name=f"h_codes_{b}_{s}", align_bytes=64)
+                h_planes[b, s] = keep.tile([P, 512], U8, name=f"h_planes_{b}_{s}", align_bytes=64)
+
+        def quantize_h(b, s, c0, n):
+            nc.vector.quantize_mx(
+                out=h_codes[b, s][:, c0 : c0 + n].bitcast(FP8X4),
+                scales=h_planes[b, s][:, c0 : c0 + n],
+                in_=h_grouped[b, s][:, c0 : c0 + n, :].rearrange("p n j -> p (n j)"),
+            )
+
+        def narrow_slice(b, s):
+            for g in range(4):
+                bank = psum.tile([P, 4, P], F32, name="bank")
+                for j in range(4):
+                    for a in range(KA):
+                        layer1(bank[:, j, :], b, a, j, 512 * s + P * g, P)
+                nc.scalar.activation(
+                    h_grouped[b, s][:, P * g : P * (g + 1), :], bank[:].rearrange("p j n -> p n j"), RELU
+                )
+                if g % 2 == 1:
+                    quantize_h(b, s, P * (g - 1), 2 * P)
+
+        def wide_banks():
+            return [psum.tile([P, 512], F32, name="bank") for j in range(4)]
+
+        def wide_planes(b, s, banks, on_scalar):
+            planes = ring.tile([P, 4, 512], BF16, name="planes", bufs=2)
+            for j in range(4):
+                if j < on_scalar:
+                    nc.scalar.activation(planes[:, j, :], banks[j][:], RELU)
+                else:
+                    nc.vector.tensor_scalar_max(planes[:, j, :], banks[j][:], 0.0)
+            return planes
+
+        def wide_finish(b, s, planes, on_scalar):
+            dst = h_grouped[b, s][:].rearrange("p (c i) t -> p c t i", i=4)
+            src = planes[:].rearrange("p t (c i) -> p c t i", i=4)
+            if on_scalar > 0:
+                nc.scalar.copy(dst[:, :on_scalar], src[:, :on_scalar])
+            nc.vector.tensor_copy(dst[:, on_scalar:], src[:, on_scalar:])
+            quantize_h(b, s, 0, 512)
+
+        early = wide_banks()
+        for a in range(KA):
+            grouped = lay_out_w1(0, a, P if a < 2 else 80)
+            gather_words(a, 0)
+            gather_words(a, 1)
+            if a == 0:
+                gather_scales(0)
+                gather_scales(1)
+            quantize_w1(0, a, grouped)
+            for j in range(4):
+                layer1(early[j][:], 0, a, j, 0, 512)
+        planes0 = wide_planes(0, 0, early, 4)
+        early1 = None
+        for a in range(KA):
+            grouped = lay_out_w1(1, a, (0, 0, 32)[a])
+            quantize_w1(1, a, grouped)
+            if a == 0:
+                narrow_slice(0, 1)
+                early1 = wide_banks()
+            for j in range(4):
+                layer1(early1[j][:], 1, a, j, 0, 512)
+        planes1 = wide_planes(1, 0, early1, 2)
+        wide_finish(0, 0, planes0, 64)
+        wide_finish(1, 0, planes1, 32)
+        narrow_slice(1, 1)
+
+        for s in range(NS):
+            n = 0
+            for count in ((1, 1, 2, 2, 2), (2, 2, 2, 1, 1))[s]:
+                result = ring.tile([P, count, 512], F32, name=f"result{count}", bufs=4)
+                for v in range(count):
+                    bank = psum.tile([P, 512], F32, name="bank")
+                    for b in range(HB):
+                        nc.tensor.matmul_mx(
+                            out=bank[:],
+                            lhsT=w2_codes[b][:].bitcast(U8)[:, 256 * (n + v) : 256 * (n + v + 1)].bitcast(FP4X4),
+                            lhsT_scale=w2_planes[:, b, :].bitcast(U8)[:, P * (n + v) : P * (n + v + 1)],
+                            rhs=h_codes[b, s][:].bitcast(FP8X4),
+                            rhs_scale=h_planes[b, s][:],
+                            start=(b == 0),
+                            stop=(b == HB - 1),
+                        )
+                    nc.vector.tensor_tensor(result[:, v, :], bank[:], prev_sb[s, (n + v) // 4][:, (n + v) % 4, :], ADD)
+                nc.sync.dma_start(
+                    out[P * n : P * (n + count), 512 * s : 512 * (s + 1)].rearrange("(v p) j -> p v j", p=P),
+                    result[:],
+                )
+                n += count

@@ -47,12 +47,14 @@ def tile_list_tabmlp_res_kernel(tc, tab, w1, w2_words, w2_scales, prev, offs, ou
         raw = {}
         tab_words = {}
 
-        def load_w1(b, a):
-            raw[b, a] = keep.tile([P, 4, PASS], F32, name=f"raw_{b}_{a}")
-            nc.sync.dma_start(
-                raw[b, a][:],
-                w1[PASS * a : PASS * (a + 1), PASS * b : PASS * (b + 1)].rearrange("(p j) c -> p j c", j=4),
-            )
+        def load_w1(b, a, pieces=1):
+            n = PASS // pieces
+            raw[b, a] = [keep.tile([P, 4, n], F32, name=f"raw_{b}_{a}_{i}") for i in range(pieces)]
+            for i in range(pieces):
+                c0 = PASS * b + n * i
+                nc.sync.dma_start(
+                    raw[b, a][i][:], w1[PASS * a : PASS * (a + 1), c0 : c0 + n].rearrange("(p j) c -> p j c", j=4)
+                )
 
         def load_tab(a):
             tab_words[a] = keep.tile([P, T], I32, name=f"tab_words_{a}")
@@ -60,19 +62,19 @@ def tile_list_tabmlp_res_kernel(tc, tab, w1, w2_words, w2_scales, prev, offs, ou
                 tab_words[a][:], tab[a, 0 : PASS * T].rearrange("(p x) -> p x", p=P).bitcast(I32)
             )
 
-        load_w1(0, 0)
         load_tab(0)
+        load_w1(0, 0)
         for q in range(4):
             nc.sync.dma_start(
                 tab_scales[32 * q : 32 * q + 4 * KA, :],
                 tab_bytes[:, 4 * q : 4 * q + 4, :].bitcast(I32),
             )
-        load_w1(0, 1)
         load_tab(1)
-        load_tab(2)
+        load_w1(0, 1)
         load_w1(0, 2)
+        load_tab(2)
         for a in range(KA):
-            load_w1(1, a)
+            load_w1(1, a, 2 if a == 2 else 1)
         w2_codes = {}
         for b in range(HB):
             w2_codes[b] = keep.tile([P, M // 2], I32, name=f"w2_codes_{b}", align_bytes=64)
@@ -96,12 +98,15 @@ def tile_list_tabmlp_res_kernel(tc, tab, w1, w2_words, w2_scales, prev, offs, ou
 
         def lay_out_w1(b, a, on_scalar):
             grouped = ring.tile([P, 4, P, 4], BF16, name="grouped", align_bytes=64)
-            src = raw[b, a][:].rearrange("p j (m t) -> p m j t", t=4)
-            dst = grouped[:].rearrange("p t m j -> p m j t")
-            if on_scalar > 0:
-                nc.scalar.copy(dst[:, :on_scalar], src[:, :on_scalar])
-            if on_scalar < P:
-                nc.vector.tensor_copy(dst[:, on_scalar:], src[:, on_scalar:])
+            pieces = raw[b, a]
+            n = P // len(pieces)
+            for i in range(len(pieces)):
+                src = pieces[i][:].rearrange("p j (m t) -> p m j t", t=4)
+                dst = grouped[:, :, n * i : n * (i + 1), :].rearrange("p t m j -> p m j t")
+                if on_scalar:
+                    nc.scalar.copy(dst, src)
+                else:
+                    nc.vector.tensor_copy(dst, src)
             return grouped
 
         def quantize_w1(b, a, grouped):
@@ -159,7 +164,7 @@ def tile_list_tabmlp_res_kernel(tc, tab, w1, w2_words, w2_scales, prev, offs, ou
                 in_=h_grouped[b, s][:, c0 : c0 + n, :].rearrange("p n j -> p (n j)"),
             )
 
-        def narrow_slice(b, s):
+        def narrow_slice(b, s, quantize):
             for g in range(4):
                 bank = psum.tile([P, 4, P], F32, name="bank")
                 for j in range(4):
@@ -168,7 +173,7 @@ def tile_list_tabmlp_res_kernel(tc, tab, w1, w2_words, w2_scales, prev, offs, ou
                 nc.scalar.activation(
                     h_grouped[b, s][:, P * g : P * (g + 1), :], bank[:].rearrange("p j n -> p n j"), RELU
                 )
-                if g % 2 == 1:
+                if quantize and g % 2 == 1:
                     quantize_h(b, s, P * (g - 1), 2 * P)
 
         def wide_banks():
@@ -183,44 +188,51 @@ def tile_list_tabmlp_res_kernel(tc, tab, w1, w2_words, w2_scales, prev, offs, ou
                     nc.vector.tensor_scalar_max(planes[:, j, :], banks[j][:], 0.0)
             return planes
 
-        def wide_finish(b, s, planes, on_scalar):
-            dst = h_grouped[b, s][:].rearrange("p (c i) t -> p c t i", i=4)
-            src = planes[:].rearrange("p t (c i) -> p c t i", i=4)
-            if on_scalar > 0:
-                nc.scalar.copy(dst[:, :on_scalar], src[:, :on_scalar])
-            nc.vector.tensor_copy(dst[:, on_scalar:], src[:, on_scalar:])
+        def wide_finish(b, s, planes, engines):
+            for g in range(4):
+                cols = slice(P * g, P * (g + 1))
+                dst = h_grouped[b, s][:, cols, :].rearrange("p (c i) t -> p c t i", i=4)
+                src = planes[:, :, cols].rearrange("p t (c i) -> p c t i", i=4)
+                if engines[g] == "S":
+                    nc.scalar.copy(dst, src)
+                else:
+                    nc.vector.tensor_copy(dst, src)
             quantize_h(b, s, 0, 512)
 
         early = wide_banks()
         for a in range(KA):
-            grouped = lay_out_w1(0, a, P if a < 2 else 80)
+            if a == 2:
+                quantize_w1(0, a, lay_out_w1(0, a, True))
             gather_words(a, 0)
-            gather_words(a, 1)
+            if a < 2:
+                gather_words(a, 1)
             if a == 0:
                 gather_scales(0)
                 gather_scales(1)
-            quantize_w1(0, a, grouped)
+            if a < 2:
+                quantize_w1(0, a, lay_out_w1(0, a, True))
             for j in range(4):
                 layer1(early[j][:], 0, a, j, 0, 512)
+        gather_words(2, 1)
         planes0 = wide_planes(0, 0, early, 4)
         early1 = None
         for a in range(KA):
-            grouped = lay_out_w1(1, a, (0, 0, 32)[a])
-            quantize_w1(1, a, grouped)
+            quantize_w1(1, a, lay_out_w1(1, a, a == 0))
             if a == 0:
-                narrow_slice(0, 1)
+                narrow_slice(0, 1, False)
                 early1 = wide_banks()
             for j in range(4):
                 layer1(early1[j][:], 1, a, j, 0, 512)
         planes1 = wide_planes(1, 0, early1, 2)
-        wide_finish(0, 0, planes0, 64)
-        wide_finish(1, 0, planes1, 32)
-        narrow_slice(1, 1)
+        wide_finish(1, 0, planes1, "VSVV")
+        wide_finish(0, 0, planes0, "VSVS")
+        quantize_h(0, 1, 0, 512)
+        narrow_slice(1, 1, True)
 
         for s in range(NS):
             n = 0
             for count in ((1, 1, 2, 2, 2), (2, 2, 2, 1, 1))[s]:
-                result = ring.tile([P, count, 512], F32, name=f"result{count}", bufs=4)
+                result = ring.tile([P, count, 512], F32, name=f"result{count}", bufs=4 if count == 1 else 6)
                 for v in range(count):
                     bank = psum.tile([P, 512], F32, name="bank")
                     for b in range(HB):
@@ -233,7 +245,8 @@ def tile_list_tabmlp_res_kernel(tc, tab, w1, w2_words, w2_scales, prev, offs, ou
                             start=(b == 0),
                             stop=(b == HB - 1),
                         )
-                    nc.vector.tensor_tensor(result[:, v, :], bank[:], prev_sb[s, (n + v) // 4][:, (n + v) % 4, :], ADD)
+                    residual = prev_sb[s, (n + v) // 4][:, (n + v) % 4, :]
+                    nc.vector.tensor_tensor(result[:, v, :], bank[:], residual, ADD)
                 nc.sync.dma_start(
                     out[P * n : P * (n + count), 512 * s : 512 * (s + 1)].rearrange("(v p) j -> p v j", p=P),
                     result[:],

@@ -22,14 +22,15 @@ KA = K // PASS
 HB = H // PASS
 NS = S // 512
 NT = M // P
+PASSES = ((1,0,2), (0,1,2))
 
 
 def tile_list_tabmlp_res_kernel(tc, tab, w1, w2_words, w2_scales, prev, offs, out):
     nc = tc.nc
     with ExitStack() as ctx:
         keep = ctx.enter_context(tc.tile_pool(name="keep", bufs=1))
-        ring = ctx.enter_context(tc.tile_pool(name="ring", bufs=3))
-        psum = ctx.enter_context(tc.psum_pool(name="psum", bufs=8))
+        ring = ctx.enter_context(tc.tile_pool(name="ring", bufs=1))
+        psum = ctx.enter_context(tc.psum_pool(name="psum", bufs=1))
 
         offsets = keep.tile([P, S // 16], U16, name="offsets")
         nc.sync.dma_start(offsets[:], offs)
@@ -43,18 +44,18 @@ def tile_list_tabmlp_res_kernel(tc, tab, w1, w2_words, w2_scales, prev, offs, ou
         nc.scalar.activation(warm[:], warm[:], RELU)
 
         tab_bytes = tab[:, PASS * T :].rearrange("a (q t) -> a q t", t=T)
+        for q in range(4):
+            nc.gpsimd.dma_start(
+                tab_scales[32 * q : 32 * q + 4 * KA, :],
+                tab_bytes[:, 4 * q : 4 * q + 4, :].bitcast(I32),
+            )
+        for q in range(4):
+            nc.gpsimd.dma_start(
+                w2_planes[32 * q : 32 * q + 4, :, :],
+                w2_scales[:, 4 * q : 4 * q + 4, :].rearrange("b q n -> q b n").bitcast(I32),
+            )
 
-        raw = {}
         tab_words = {}
-
-        def load_w1(b, a, pieces=1):
-            n = PASS // pieces
-            raw[b, a] = [keep.tile([P, 4, n], F32, name=f"raw_{b}_{a}_{i}") for i in range(pieces)]
-            for i in range(pieces):
-                c0 = PASS * b + n * i
-                nc.sync.dma_start(
-                    raw[b, a][i][:], w1[PASS * a : PASS * (a + 1), c0 : c0 + n].rearrange("(p j) c -> p j c", j=4)
-                )
 
         def load_tab(a):
             tab_words[a] = keep.tile([P, T], I32, name=f"tab_words_{a}")
@@ -62,48 +63,54 @@ def tile_list_tabmlp_res_kernel(tc, tab, w1, w2_words, w2_scales, prev, offs, ou
                 tab_words[a][:], tab[a, 0 : PASS * T].rearrange("(p x) -> p x", p=P).bitcast(I32)
             )
 
-        load_tab(0)
-        load_w1(0, 0)
-        for q in range(4):
+        def load_w1(a, c0, n):
+            raw = keep.tile([P, 4, n], F32, name=f"raw_{a}_{c0}")
             nc.sync.dma_start(
-                tab_scales[32 * q : 32 * q + 4 * KA, :],
-                tab_bytes[:, 4 * q : 4 * q + 4, :].bitcast(I32),
+                raw[:], w1[PASS * a : PASS * (a + 1), c0 : c0 + n].rearrange("(p j) c -> p j c", j=4)
             )
+            return raw
+
+        pieces = {}
+
+        def load_block(b, a):
+            raw = load_w1(a, PASS * b, PASS)
+            pieces[b, a] = [raw[:, :, 256 * i : 256 * (i + 1)] for i in range(2)]
+
+        def load_halves(b, a):
+            pieces[b, a] = [load_w1(a, PASS * b + 256 * i, 256)[:] for i in range(2)]
+
+        def load_rows(a):
+            raw = load_w1(a, 0, H)
+            for b in range(HB):
+                pieces[b, a] = [raw[:, :, PASS * b + 256 * i : PASS * b + 256 * (i + 1)] for i in range(2)]
+
         load_tab(1)
-        load_w1(0, 1)
-        load_w1(0, 2)
+        load_tab(0)
+        load_block(0, 0)
+        load_block(0, 1)
+        load_block(0, 2)
         load_tab(2)
-        for a in range(KA):
-            load_w1(1, a, 2 if a == 2 else 1)
+        load_block(1, 0)
+        load_block(1, 1)
+        load_halves(1, 2)
         w2_codes = {}
         for b in range(HB):
             w2_codes[b] = keep.tile([P, M // 2], I32, name=f"w2_codes_{b}", align_bytes=64)
             nc.sync.dma_start(w2_codes[b][:], w2_words[b].bitcast(I32))
-        for q in range(4):
-            nc.sync.dma_start(
-                w2_planes[32 * q : 32 * q + 4, :, :],
-                w2_scales[:, 4 * q : 4 * q + 4, :].rearrange("b q n -> q b n").bitcast(I32),
-            )
-        prev_sb = {}
-        for s in range(NS):
-            for u in range(2):
-                prev_sb[s, u] = keep.tile([P, 4, 512], F32, name=f"prev_{s}_{u}")
-                nc.sync.dma_start(
-                    prev_sb[s, u][:],
-                    prev[512 * u : 512 * (u + 1), 512 * s : 512 * (s + 1)].rearrange("(t p) j -> p t j", p=P),
-                )
+        prev_sb = []
+        for u in range(NT // 2):
+            prev_sb.append(keep.tile([P, 2, S], F32, name=f"prev_{u}"))
+            nc.sync.dma_start(prev_sb[u][:], prev[256 * u : 256 * (u + 1), :].rearrange("(t p) j -> p t j", p=P))
 
         w1_codes = {}
         w1_planes = {}
 
-        def lay_out_w1(b, a, on_scalar):
-            grouped = ring.tile([P, 4, P, 4], BF16, name="grouped", align_bytes=64)
-            pieces = raw[b, a]
-            n = P // len(pieces)
-            for i in range(len(pieces)):
-                src = pieces[i][:].rearrange("p j (m t) -> p m j t", t=4)
-                dst = grouped[:, :, n * i : n * (i + 1), :].rearrange("p t m j -> p m j t")
-                if on_scalar:
+        def lay_out_w1(b, a, engines):
+            grouped = ring.tile([P, 4, P, 4], BF16, name=f"grouped_{a}", align_bytes=64)
+            for i in range(2):
+                src = pieces[b, a][i].rearrange("p j (m t) -> p m j t", t=4)
+                dst = grouped[:, :, 64 * i : 64 * (i + 1), :].rearrange("p t m j -> p m j t")
+                if engines[i] == "S":
                     nc.scalar.copy(dst, src)
                 else:
                     nc.vector.tensor_copy(dst, src)
@@ -142,8 +149,8 @@ def tile_list_tabmlp_res_kernel(tc, tab, w1, w2_words, w2_scales, prev, offs, ou
                 lhsT_scale=w1_planes[b, a][:, P * j : P * (j + 1)],
                 rhs=picked[a][:, t0 : t0 + n].bitcast(FP8X4),
                 rhs_scale=picked_scales[4 * a : P, t0 : t0 + n],
-                start=(a == 0),
-                stop=(a == KA - 1),
+                start=(a == PASSES[b][0]),
+                stop=(a == PASSES[b][-1]),
             )
 
         h_grouped = {}
@@ -164,28 +171,29 @@ def tile_list_tabmlp_res_kernel(tc, tab, w1, w2_words, w2_scales, prev, offs, ou
                 in_=h_grouped[b, s][:, c0 : c0 + n, :].rearrange("p n j -> p (n j)"),
             )
 
-        def narrow_slice(b, s, quantize):
+        def relu(dst, src, engine):
+            if engine == "S":
+                nc.scalar.activation(dst, src, RELU)
+            else:
+                nc.vector.tensor_scalar_max(dst, src, 0.0)
+
+        def narrow_slice(b, s, quantize, engines, first):
             for g in range(4):
-                bank = psum.tile([P, 4, P], F32, name="bank")
+                bank = psum.tile([P, 4, P], F32, name=f"bank{first + g}")
                 for j in range(4):
-                    for a in range(KA):
+                    for a in PASSES[b]:
                         layer1(bank[:, j, :], b, a, j, 512 * s + P * g, P)
-                nc.scalar.activation(
-                    h_grouped[b, s][:, P * g : P * (g + 1), :], bank[:].rearrange("p j n -> p n j"), RELU
-                )
+                relu(h_grouped[b, s][:, P * g : P * (g + 1), :], bank[:].rearrange("p j n -> p n j"), engines[g])
                 if quantize and g % 2 == 1:
                     quantize_h(b, s, P * (g - 1), 2 * P)
 
-        def wide_banks():
-            return [psum.tile([P, 512], F32, name="bank") for j in range(4)]
+        def wide_banks(first):
+            return [psum.tile([P, 512], F32, name=f"bank{first + j}") for j in range(4)]
 
-        def wide_planes(b, s, banks, on_scalar):
-            planes = ring.tile([P, 4, 512], BF16, name="planes", bufs=2)
+        def wide_planes(b, s, banks, engines):
+            planes = ring.tile([P, 4, 512], BF16, name=f"planes_{b}")
             for j in range(4):
-                if j < on_scalar:
-                    nc.scalar.activation(planes[:, j, :], banks[j][:], RELU)
-                else:
-                    nc.vector.tensor_scalar_max(planes[:, j, :], banks[j][:], 0.0)
+                relu(planes[:, j, :], banks[j][:], engines[j])
             return planes
 
         def wide_finish(b, s, planes, engines):
@@ -199,42 +207,50 @@ def tile_list_tabmlp_res_kernel(tc, tab, w1, w2_words, w2_scales, prev, offs, ou
                     nc.vector.tensor_copy(dst, src)
             quantize_h(b, s, 0, 512)
 
-        early = wide_banks()
-        for a in range(KA):
-            if a == 2:
-                quantize_w1(0, a, lay_out_w1(0, a, True))
-            gather_words(a, 0)
-            if a < 2:
-                gather_words(a, 1)
-            if a == 0:
-                gather_scales(0)
-                gather_scales(1)
-            if a < 2:
-                quantize_w1(0, a, lay_out_w1(0, a, True))
-            for j in range(4):
-                layer1(early[j][:], 0, a, j, 0, 512)
+        gather_words(2, 0)
+        gather_scales(0)
+        gather_words(0, 1)
+        gather_words(1, 0)
+        gather_words(1, 1)
+        quantize_w1(0, 1, lay_out_w1(0, 1, "SV"))
+        gather_scales(1)
+        gather_words(0, 0)
+        quantize_w1(0, 0, lay_out_w1(0, 0, "SS"))
+        quantize_w1(1, 0, lay_out_w1(1, 0, "VV"))
+        early0 = wide_banks(0)
+        for j in range(4):
+            layer1(early0[j][:], 0, 1, j, 0, 512)
+        quantize_w1(0, 2, lay_out_w1(0, 2, "SV"))
+        for j in range(4):
+            layer1(early0[j][:], 0, 0, j, 0, 512)
+        quantize_w1(1, 1, lay_out_w1(1, 1, "VV"))
+        early1 = wide_banks(4)
+        for j in range(4):
+            layer1(early1[j][:], 1, 0, j, 0, 512)
+        for j in range(4):
+            layer1(early0[j][:], 0, 2, j, 0, 512)
+        quantize_w1(1, 2, lay_out_w1(1, 2, "VV"))
+        for j in range(4):
+            layer1(early1[j][:], 1, 1, j, 0, 512)
         gather_words(2, 1)
-        planes0 = wide_planes(0, 0, early, 4)
-        early1 = None
-        for a in range(KA):
-            quantize_w1(1, a, lay_out_w1(1, a, a == 0))
-            if a == 0:
-                narrow_slice(0, 1, False)
-                early1 = wide_banks()
-            for j in range(4):
-                layer1(early1[j][:], 1, a, j, 0, 512)
-        planes1 = wide_planes(1, 0, early1, 2)
-        wide_finish(1, 0, planes1, "VSVV")
-        wide_finish(0, 0, planes0, "VSVS")
+        planes0 = wide_planes(0, 0, early0, "SSSS")
+        for j in range(4):
+            layer1(early1[j][:], 1, 2, j, 0, 512)
+        narrow_slice(0, 1, False, "SSSS", 0)
+        planes1 = wide_planes(1, 0, early1, "VSVS")
+        wide_finish(1, 0, planes1, "SVSV")
+        narrow_slice(1, 1, True, "VSSS", 0)
+        wide_finish(0, 0, planes0, "SSSS")
         quantize_h(0, 1, 0, 512)
-        narrow_slice(1, 1, True)
 
         for s in range(NS):
+            cols = slice(512 * s, 512 * (s + 1))
             n = 0
             for count in ((1, 1, 2, 2, 2), (2, 2, 2, 1, 1))[s]:
-                result = ring.tile([P, count, 512], F32, name=f"result{count}", bufs=4 if count == 1 else 6)
+                result = keep.tile([P, count, 512], F32, name=f"result_{s}_{n}")
                 for v in range(count):
-                    bank = psum.tile([P, 512], F32, name="bank")
+                    turn = 7 + NT * s + n + v
+                    bank = psum.tile([P, 512], F32, name=f"bank{turn % 8}")
                     for b in range(HB):
                         nc.tensor.matmul_mx(
                             out=bank[:],
@@ -245,10 +261,11 @@ def tile_list_tabmlp_res_kernel(tc, tab, w1, w2_words, w2_scales, prev, offs, ou
                             start=(b == 0),
                             stop=(b == HB - 1),
                         )
-                    residual = prev_sb[s, (n + v) // 4][:, (n + v) % 4, :]
-                    nc.vector.tensor_tensor(result[:, v, :], bank[:], residual, ADD)
+                    nc.vector.tensor_tensor(
+                        result[:, v, :], bank[:], prev_sb[(n + v) // 2][:, (n + v) % 2, cols], ADD
+                    )
                 nc.sync.dma_start(
-                    out[P * n : P * (n + count), 512 * s : 512 * (s + 1)].rearrange("(v p) j -> p v j", p=P),
+                    out[P * n : P * (n + count), cols].rearrange("(v p) j -> p v j", p=P),
                     result[:],
                 )
                 n += count

@@ -44,16 +44,6 @@ def tile_list_tabmlp_res_kernel(tc, tab, w1, w2_words, w2_scales, prev, offs, ou
         nc.scalar.activation(warm[:], warm[:], RELU)
 
         tab_bytes = tab[:, PASS * T :].rearrange("a (q t) -> a q t", t=T)
-        for q in range(4):
-            nc.gpsimd.dma_start(
-                tab_scales[32 * q : 32 * q + 4 * KA, :],
-                tab_bytes[:, 4 * q : 4 * q + 4, :].bitcast(I32),
-            )
-        for q in range(4):
-            nc.gpsimd.dma_start(
-                w2_planes[32 * q : 32 * q + 4, :, :],
-                w2_scales[:, 4 * q : 4 * q + 4, :].rearrange("b q n -> q b n").bitcast(I32),
-            )
 
         tab_words = {}
 
@@ -86,17 +76,27 @@ def tile_list_tabmlp_res_kernel(tc, tab, w1, w2_words, w2_scales, prev, offs, ou
 
         load_tab(1)
         load_tab(0)
-        load_block(0, 0)
+        for q in range(4):
+            nc.sync.dma_start(
+                tab_scales[32 * q : 32 * q + 4 * KA, :],
+                tab_bytes[:, 4 * q : 4 * q + 4, :].bitcast(I32),
+            )
         load_block(0, 1)
+        load_block(0, 0)
         load_block(0, 2)
         load_tab(2)
         load_block(1, 0)
         load_block(1, 1)
-        load_halves(1, 2)
+        load_block(1, 2)
         w2_codes = {}
         for b in range(HB):
             w2_codes[b] = keep.tile([P, M // 2], I32, name=f"w2_codes_{b}", align_bytes=64)
             nc.sync.dma_start(w2_codes[b][:], w2_words[b].bitcast(I32))
+        for q in range(4):
+            nc.sync.dma_start(
+                w2_planes[32 * q : 32 * q + 4, :, :],
+                w2_scales[:, 4 * q : 4 * q + 4, :].rearrange("b q n -> q b n").bitcast(I32),
+            )
         prev_sb = []
         for u in range(NT // 2):
             prev_sb.append(keep.tile([P, 2, S], F32, name=f"prev_{u}"))
@@ -207,65 +207,60 @@ def tile_list_tabmlp_res_kernel(tc, tab, w1, w2_words, w2_scales, prev, offs, ou
                     nc.vector.tensor_copy(dst, src)
             quantize_h(b, s, 0, 512)
 
+        quantize_w1(0, 0, lay_out_w1(0, 0, "VS"))
+        gather_words(0, 1)
+        quantize_w1(0, 1, lay_out_w1(0, 1, "SS"))
+        quantize_w1(1, 1, lay_out_w1(1, 1, "SV"))
         gather_words(2, 0)
         gather_scales(0)
-        gather_words(0, 1)
-        gather_words(1, 0)
-        gather_words(1, 1)
-        quantize_w1(0, 1, lay_out_w1(0, 1, "SV"))
-        gather_scales(1)
+        quantize_w1(0, 2, lay_out_w1(0, 2, "SV"))
         gather_words(0, 0)
-        quantize_w1(0, 0, lay_out_w1(0, 0, "SS"))
-        quantize_w1(1, 0, lay_out_w1(1, 0, "VV"))
-        early0 = wide_banks(0)
+        quantize_w1(1, 2, lay_out_w1(1, 2, "VS"))
+        gather_words(1, 0)
+        early0 = wide_banks(4)
         for j in range(4):
             layer1(early0[j][:], 0, 1, j, 0, 512)
-        quantize_w1(0, 2, lay_out_w1(0, 2, "SV"))
         for j in range(4):
             layer1(early0[j][:], 0, 0, j, 0, 512)
-        quantize_w1(1, 1, lay_out_w1(1, 1, "VV"))
+        for j in range(4):
+            layer1(early0[j][:], 0, 2, j, 0, 512)
+        gather_words(1, 1)
+        gather_words(2, 1)
+        planes0 = wide_planes(0, 0, early0, "SSSV")
+        gather_scales(1)
+        quantize_w1(1, 0, lay_out_w1(1, 0, "VV"))
         early1 = wide_banks(4)
         for j in range(4):
             layer1(early1[j][:], 1, 0, j, 0, 512)
         for j in range(4):
-            layer1(early0[j][:], 0, 2, j, 0, 512)
-        quantize_w1(1, 2, lay_out_w1(1, 2, "VV"))
-        for j in range(4):
             layer1(early1[j][:], 1, 1, j, 0, 512)
-        gather_words(2, 1)
-        planes0 = wide_planes(0, 0, early0, "SSSS")
         for j in range(4):
             layer1(early1[j][:], 1, 2, j, 0, 512)
-        narrow_slice(0, 1, False, "SSSS", 0)
-        planes1 = wide_planes(1, 0, early1, "VSVS")
-        wide_finish(1, 0, planes1, "SVSV")
+        planes1 = wide_planes(1, 0, early1, "SSSV")
+        narrow_slice(0, 1, False, "SSSV", 0)
         narrow_slice(1, 1, True, "VSSS", 0)
-        wide_finish(0, 0, planes0, "SSSS")
+        wide_finish(1, 0, planes1, "VVVS")
         quantize_h(0, 1, 0, 512)
+        wide_finish(0, 0, planes0, "VSVS")
 
-        for s in range(NS):
-            cols = slice(512 * s, 512 * (s + 1))
-            n = 0
-            for count in ((1, 1, 2, 2, 2), (2, 2, 2, 1, 1))[s]:
-                result = keep.tile([P, count, 512], F32, name=f"result_{s}_{n}")
-                for v in range(count):
-                    turn = 7 + NT * s + n + v
-                    bank = psum.tile([P, 512], F32, name=f"bank{turn % 8}")
-                    for b in range(HB):
-                        nc.tensor.matmul_mx(
-                            out=bank[:],
-                            lhsT=w2_codes[b][:].bitcast(U8)[:, 256 * (n + v) : 256 * (n + v + 1)].bitcast(FP4X4),
-                            lhsT_scale=w2_planes[:, b, :].bitcast(U8)[:, P * (n + v) : P * (n + v + 1)],
-                            rhs=h_codes[b, s][:].bitcast(FP8X4),
-                            rhs_scale=h_planes[b, s][:],
-                            start=(b == 0),
-                            stop=(b == HB - 1),
-                        )
-                    nc.vector.tensor_tensor(
-                        result[:, v, :], bank[:], prev_sb[(n + v) // 2][:, (n + v) % 2, cols], ADD
+        for n in range(NT):
+            result = keep.tile([P, S], F32, name=f"result_{n}")
+            for s in range(NS):
+                turn = 6 + 2 * n + s
+                cols = slice(512 * s, 512 * (s + 1))
+                bank = psum.tile([P, 512], F32, name=f"bank{turn % 8}")
+                for b in range(HB):
+                    nc.tensor.matmul_mx(
+                        out=bank[:],
+                        lhsT=w2_codes[b][:].bitcast(U8)[:, 256 * n : 256 * (n + 1)].bitcast(FP4X4),
+                        lhsT_scale=w2_planes[:, b, :].bitcast(U8)[:, P * n : P * (n + 1)],
+                        rhs=h_codes[b, s][:].bitcast(FP8X4),
+                        rhs_scale=h_planes[b, s][:],
+                        start=(b == 0),
+                        stop=(b == HB - 1),
                     )
-                nc.sync.dma_start(
-                    out[P * n : P * (n + count), cols].rearrange("(v p) j -> p v j", p=P),
-                    result[:],
-                )
-                n += count
+                nc.vector.tensor_tensor(result[:, cols], bank[:], prev_sb[n // 2][:, n % 2, cols], ADD)
+                if n == NT - 1:
+                    nc.sync.dma_start(out[P * n : P * (n + 1), cols], result[:, cols])
+            if n < NT - 1:
+                nc.sync.dma_start(out[P * n : P * (n + 1), :], result[:])

from contextlib import ExitStack

import concourse.mybir as mybir

K, H, M, T, S = 1536, 1024, 1024, 2048, 1024
FLOPS = 2 * K * H * S + 2 * H * M * S

F32 = mybir.dt.float32
BF16 = mybir.dt.bfloat16
I32 = mybir.dt.int32
U32 = mybir.dt.uint32
U16 = mybir.dt.uint16
U8 = mybir.dt.uint8
FP8X4 = mybir.dt.float8_e4m3fn_x4
FP4X4 = mybir.dt.float4_e2m1fn_x4
RELU = mybir.ActivationFunctionType.Relu
ADD = mybir.AluOpType.add

P = 128
PASS = 512
KA = K // PASS
HB = H // PASS
NS = S // 512
NT = M // P
PASSES = ((1,0,2), (0,1,2))


def tile_list_tabmlp_res_kernel(tc, tab, w1, w2_words, w2_scales, prev, offs, out):
    nc = tc.nc
    with ExitStack() as ctx:
        keep = ctx.enter_context(tc.tile_pool(name="keep", bufs=1))
        ring = ctx.enter_context(tc.tile_pool(name="ring", bufs=1))
        psum = ctx.enter_context(tc.psum_pool(name="psum", bufs=1))

        offsets = keep.tile([P, S // 16], U16, name="offsets")
        nc.sync.dma_start(offsets[:], offs)

        tab_scales = keep.tile([P, T // 4], I32, name="tab_scales", align_bytes=64)
        nc.vector.memset(tab_scales[:], 0)
        w2_planes = keep.tile([P, HB, M // 4], I32, name="w2_planes", align_bytes=64)
        nc.vector.memset(w2_planes[:], 0)
        warm = keep.tile([P, 1], F32, name="warm")
        nc.vector.memset(warm[:], 0.0)
        nc.scalar.activation(warm[:], warm[:], RELU)

        tab_bytes = tab[:, PASS * T :].rearrange("a (q t) -> a q t", t=T)

        tab_words = {}

        def load_tab(a):
            tab_words[a] = keep.tile([P, T], I32, name=f"tab_words_{a}")
            nc.sync.dma_start(
                tab_words[a][:], tab[a, 0 : PASS * T].rearrange("(p x) -> p x", p=P).bitcast(I32)
            )

        def load_w1(a, c0, n):
            raw = keep.tile([P, 4, n], F32, name=f"raw_{a}_{c0}")
            nc.sync.dma_start(
                raw[:], w1[PASS * a : PASS * (a + 1), c0 : c0 + n].rearrange("(p j) c -> p j c", j=4)
            )
            return raw

        pieces = {}

        def load_block(b, a):
            raw = load_w1(a, PASS * b, PASS)
            pieces[b, a] = [raw[:, :, 256 * i : 256 * (i + 1)] for i in range(2)]

        def load_halves(b, a):
            pieces[b, a] = [load_w1(a, PASS * b + 256 * i, 256)[:] for i in range(2)]

        def load_rows(a):
            raw = load_w1(a, 0, H)
            for b in range(HB):
                pieces[b, a] = [raw[:, :, PASS * b + 256 * i : PASS * b + 256 * (i + 1)] for i in range(2)]

        load_tab(1)
        load_tab(0)
        for q in range(4):
            nc.sync.dma_start(
                tab_scales[32 * q : 32 * q + 4 * KA, :],
                tab_bytes[:, 4 * q : 4 * q + 4, :].bitcast(I32),
            )
        load_block(0, 1)
        load_block(0, 0)
        load_block(0, 2)
        load_tab(2)
        load_block(1, 0)
        load_block(1, 1)
        load_block(1, 2)
        w2_codes = {}
        for b in range(HB):
            w2_codes[b] = keep.tile([P, M // 2], I32, name=f"w2_codes_{b}", align_bytes=64)
            nc.sync.dma_start(w2_codes[b][:], w2_words[b].bitcast(I32))
        for q in range(4):
            nc.sync.dma_start(
                w2_planes[32 * q : 32 * q + 4, :, :],
                w2_scales[:, 4 * q : 4 * q + 4, :].rearrange("b q n -> q b n").bitcast(I32),
            )
        prev_sb = []
        for u in range(NT // 2):
            prev_sb.append(keep.tile([P, 2, S], F32, name=f"prev_{u}"))
            nc.sync.dma_start(prev_sb[u][:], prev[256 * u : 256 * (u + 1), :].rearrange("(t p) j -> p t j", p=P))

        w1_codes = {}
        w1_planes = {}

        def lay_out_w1(b, a, engines):
            grouped = ring.tile([P, 4, P, 4], BF16, name=f"grouped_{a}", align_bytes=64)
            for i in range(2):
                src = pieces[b, a][i].rearrange("p j (m t) -> p m j t", t=4)
                dst = grouped[:, :, 64 * i : 64 * (i + 1), :].rearrange("p t m j -> p m j t")
                if engines[i] == "S":
                    nc.scalar.copy(dst, src)
                else:
                    nc.vector.tensor_copy(dst, src)
            return grouped

        def quantize_w1(b, a, grouped):
            w1_codes[b, a] = keep.tile([P, PASS], U32, name=f"w1_codes_{b}_{a}", align_bytes=64)
            w1_planes[b, a] = keep.tile([P, PASS], U8, name=f"w1_planes_{b}_{a}", align_bytes=64)
            nc.vector.quantize_mx(
                out=w1_codes[b, a][:].bitcast(FP8X4),
                scales=w1_planes[b, a][:],
                in_=grouped[:].rearrange("p t m j -> p (t m j)"),
            )

        picked = {}
        picked_scales = keep.tile([P, S], U8, name="picked_scales", align_bytes=64)

        def gather_words(a, s):
            if a not in picked:
                picked[a] = keep.tile([P, S], U32, name=f"picked_{a}", align_bytes=64)
            nc.vector.tensor_copy(
                picked[a][:, 512 * s : 512 * (s + 1)],
                tab_words[a][:].bitcast(U32).indirect(offsets[:, 32 * s : 32 * (s + 1)]),
            )

        def gather_scales(s):
            nc.vector.tensor_copy(
                picked_scales[:, 512 * s : 512 * (s + 1)],
                tab_scales[:].bitcast(U8).indirect(offsets[:, 32 * s : 32 * (s + 1)]),
            )

        def layer1(dst, b, a, j, t0, n):
            nc.tensor.matmul_mx(
                out=dst,
                lhsT=w1_codes[b, a][:, P * j : P * (j + 1)].bitcast(FP8X4),
                lhsT_scale=w1_planes[b, a][:, P * j : P * (j + 1)],
                rhs=picked[a][:, t0 : t0 + n].bitcast(FP8X4),
                rhs_scale=picked_scales[4 * a : P, t0 : t0 + n],
                start=(a == PASSES[b][0]),
                stop=(a == PASSES[b][-1]),
            )

        h_grouped = {}
        for b in range(HB):
            for s in range(NS):
                h_grouped[b, s] = keep.tile([P, 512, 4], BF16, name=f"h_grouped_{b}_{s}", align_bytes=64)
        h_codes = {}
        h_planes = {}
        for b in range(HB):
            for s in range(NS):
                h_codes[b, s] = keep.tile([P, 512], U32, name=f"h_codes_{b}_{s}", align_bytes=64)
                h_planes[b, s] = keep.tile([P, 512], U8, name=f"h_planes_{b}_{s}", align_bytes=64)

        def quantize_h(b, s, c0, n):
            nc.vector.quantize_mx(
                out=h_codes[b, s][:, c0 : c0 + n].bitcast(FP8X4),
                scales=h_planes[b, s][:, c0 : c0 + n],
                in_=h_grouped[b, s][:, c0 : c0 + n, :].rearrange("p n j -> p (n j)"),
            )

        def relu(dst, src, engine):
            if engine == "S":
                nc.scalar.activation(dst, src, RELU)
            else:
                nc.vector.tensor_scalar_max(dst, src, 0.0)

        def narrow_slice(b, s, quantize, engines, first):
            for g in range(4):
                bank = psum.tile([P, 4, P], F32, name=f"bank{first + g}")
                for j in range(4):
                    for a in PASSES[b]:
                        layer1(bank[:, j, :], b, a, j, 512 * s + P * g, P)
                relu(h_grouped[b, s][:, P * g : P * (g + 1), :], bank[:].rearrange("p j n -> p n j"), engines[g])
                if quantize and g % 2 == 1:
                    quantize_h(b, s, P * (g - 1), 2 * P)

        def wide_banks(first):
            return [psum.tile([P, 512], F32, name=f"bank{first + j}") for j in range(4)]

        def wide_planes(b, s, banks, engines):
            planes = ring.tile([P, 4, 512], BF16, name=f"planes_{b}")
            for j in range(4):
                relu(planes[:, j, :], banks[j][:], engines[j])
            return planes

        def wide_finish(b, s, planes, engines):
            for g in range(4):
                cols = slice(P * g, P * (g + 1))
                dst = h_grouped[b, s][:, cols, :].rearrange("p (c i) t -> p c t i", i=4)
                src = planes[:, :, cols].rearrange("p t (c i) -> p c t i", i=4)
                if engines[g] == "S":
                    nc.scalar.copy(dst, src)
                else:
                    nc.vector.tensor_copy(dst, src)
            quantize_h(b, s, 0, 512)

        quantize_w1(0, 0, lay_out_w1(0, 0, "VS"))
        gather_words(0, 1)
        quantize_w1(0, 1, lay_out_w1(0, 1, "SS"))
        quantize_w1(1, 1, lay_out_w1(1, 1, "SV"))
        gather_words(2, 0)
        gather_scales(0)
        quantize_w1(0, 2, lay_out_w1(0, 2, "SV"))
        gather_words(0, 0)
        quantize_w1(1, 2, lay_out_w1(1, 2, "VS"))
        gather_words(1, 0)
        early0 = wide_banks(4)
        for j in range(4):
            layer1(early0[j][:], 0, 1, j, 0, 512)
        for j in range(4):
            layer1(early0[j][:], 0, 0, j, 0, 512)
        for j in range(4):
            layer1(early0[j][:], 0, 2, j, 0, 512)
        gather_words(1, 1)
        gather_words(2, 1)
        planes0 = wide_planes(0, 0, early0, "SSSV")
        gather_scales(1)
        quantize_w1(1, 0, lay_out_w1(1, 0, "VV"))
        early1 = wide_banks(4)
        for j in range(4):
            layer1(early1[j][:], 1, 0, j, 0, 512)
        for j in range(4):
            layer1(early1[j][:], 1, 1, j, 0, 512)
        for j in range(4):
            layer1(early1[j][:], 1, 2, j, 0, 512)
        planes1 = wide_planes(1, 0, early1, "SSSV")
        narrow_slice(0, 1, False, "SSSV", 0)
        narrow_slice(1, 1, True, "VSSS", 0)
        wide_finish(1, 0, planes1, "VVVS")
        quantize_h(0, 1, 0, 512)
        wide_finish(0, 0, planes0, "VSVS")

        for n in range(NT):
            result = keep.tile([P, S], F32, name=f"result_{n}")
            for s in range(NS):
                turn = 6 + 2 * n + s
                cols = slice(512 * s, 512 * (s + 1))
                bank = psum.tile([P, 512], F32, name=f"bank{turn % 8}")
                for b in range(HB):
                    nc.tensor.matmul_mx(
                        out=bank[:],
                        lhsT=w2_codes[b][:].bitcast(U8)[:, 256 * n : 256 * (n + 1)].bitcast(FP4X4),
                        lhsT_scale=w2_planes[:, b, :].bitcast(U8)[:, P * n : P * (n + 1)],
                        rhs=h_codes[b, s][:].bitcast(FP8X4),
                        rhs_scale=h_planes[b, s][:],
                        start=(b == 0),
                        stop=(b == HB - 1),
                    )
                nc.vector.tensor_tensor(result[:, cols], bank[:], prev_sb[n // 2][:, n % 2, cols], ADD)
                if n == NT - 1:
                    nc.sync.dma_start(out[P * n : P * (n + 1), cols], result[:, cols])
            if n < NT - 1:
                nc.sync.dma_start(out[P * n : P * (n + 1), :], result[:])
